import numpy as np
import ml_dtypes


def mxq(x, axis, fmt="e4m3"):
    dtype, down = {"e4m3": (ml_dtypes.float8_e4m3fn, 7), "e5m2": (ml_dtypes.float8_e5m2, 14)}[fmt]
    v = np.moveaxis(np.asarray(x, np.float32).astype(ml_dtypes.bfloat16).astype(np.float64), axis, -1)
    blocks = v.reshape(v.shape[:-1] + (-1, 32))
    amax = np.abs(blocks).max(-1, keepdims=True)
    byte = np.maximum(np.where(amax > 0, np.frexp(amax)[1] - 1 + 127, 0) - down, 1)
    scale = np.exp2(byte - 127.0)
    codes = (blocks / scale).astype(np.float32).astype(dtype).astype(np.float64)
    return np.moveaxis((codes * scale).reshape(v.shape), -1, axis)


WIDE = False


def mx_kscale(k):
    if not WIDE:
        return np.ones(k)
    levels = np.array([30, -30])
    if k % 512:
        return np.exp2(np.random.permutation(np.resize(levels, k // 32))).repeat(32)
    a = np.empty((k // 512, 16))
    for p in range(k // 512):
        a[p, :8] = np.random.permutation(np.resize(levels, 8))
        for g in range(8):
            far = levels[np.abs(levels - a[p, g]) >= 10]
            a[p, g + 8] = far[np.random.randint(len(far))]
    return np.exp2(a.ravel()).repeat(32)


BF16 = ml_dtypes.bfloat16


def bf(x):
    return np.asarray(x, np.float32).astype(BF16)


def f64(x):
    return np.asarray(x).astype(np.float64)


D, U, V, T = 2048, 1024, 2048, 512

PART_STD = 0.5
UNI_RMS = np.sqrt(0.75)
BI_RMS = np.e
NOISE_TEMPERATURE = 0.5


def setup_inputs():
    s = mx_kscale(U)
    t = mx_kscale(V)
    uni = np.random.gamma(0.5, 1.0, (D, U))
    bi = np.exp(np.random.standard_normal((D, V)))
    uni_ratio = np.random.standard_normal((U, T)) * PART_STD / (UNI_RMS * np.sqrt(U))
    bi_ratio = np.random.standard_normal((V, T)) * PART_STD / (BI_RMS * np.sqrt(V))
    return {"uni_counts": bf(uni * s),
            "bi_counts": bf(bi * t),
            "uni_ratio": bf(uni_ratio / s[:, None]),
            "bi_ratio": bf(bi_ratio / t[:, None]),
            "length_gain": bf(1 + 0.1 * np.random.standard_normal(D)),
            "log_prior": bf(0.3 * np.random.standard_normal(T)),
            "gumbel": bf(NOISE_TEMPERATURE * np.random.gumbel(size=(D, T)))}


def reference(uni_counts, bi_counts, uni_ratio, bi_ratio, length_gain, log_prior, gumbel):
    cu = mxq(f64(uni_counts), 1, "e4m3")
    ru = mxq(f64(uni_ratio), 0, "e4m3")
    cb = mxq(f64(bi_counts), 1, "e5m2")
    rb = mxq(f64(bi_ratio), 0, "e4m3")
    score = (cu @ ru) + (cb @ rb)
    log_weight = score * f64(length_gain)[:, None] + f64(log_prior)
    weight = np.exp(log_weight)
    key = log_weight + f64(gumbel)
    return weight, key

@@ -1,0 +1,355 @@
+from contextlib import ExitStack
+
+import concourse.mybir as mybir
+from concourse.masks import make_identity
+
+D, U, V, T = 2048, 1024, 2048, 512
+FLOPS = 2 * D * T * (U + V)
+
+F32 = mybir.dt.float32
+BF16 = mybir.dt.bfloat16
+U32 = mybir.dt.uint32
+U8 = mybir.dt.uint8
+E4M3 = mybir.dt.float8_e4m3fn_x4
+E5M2 = mybir.dt.float8_e5m2_x4
+ADD = mybir.AluOpType.add
+MULT = mybir.AluOpType.mult
+ACT = mybir.ActivationFunctionType
+
+P = 128
+K_PASS = 512
+UNI_PASSES = U // K_PASS
+BI_PASSES = V // K_PASS
+PASSES = UNI_PASSES + BI_PASSES
+TILES = D // P
+HALF = T // 2
+
+
+def tile_dsir_importance_weights_s2_kernel(
+    tc, uni_counts, bi_counts, uni_ratio, bi_ratio, length_gain, log_prior, gumbel, weight, key
+):
+    nc = tc.nc
+    uni_v = uni_counts.rearrange("(p n) k -> p n k", n=TILES)
+    bi_v = bi_counts.rearrange("(p n) k -> p n k", n=TILES)
+    gumbel_v = gumbel.rearrange("(p n) j -> p n j", n=TILES)
+    weight_v = weight.rearrange("(p n) j -> p n j", n=TILES)
+    key_v = key.rearrange("(p n) j -> p n j", n=TILES)
+    uni_ratio_v = uni_ratio.rearrange("(g p t) j -> g p t j", p=P, t=4)
+    bi_ratio_v = bi_ratio.rearrange("(g p t) j -> g p t j", p=P, t=4)
+
+    with ExitStack() as ctx:
+        const = ctx.enter_context(tc.tile_pool(name="const", bufs=1))
+        raw = ctx.enter_context(tc.tile_pool(name="raw", bufs=1))
+        work = ctx.enter_context(tc.tile_pool(name="work", bufs=3))
+        outs = ctx.enter_context(tc.tile_pool(name="outs", bufs=3))
+        psum_x = ctx.enter_context(tc.psum_pool(name="psum_x", bufs=6))
+        psum_a = ctx.enter_context(tc.psum_pool(name="psum_a", bufs=2))
+        ctx.enter_context(tc.manual_schedule())
+
+        ident = const.tile([P, P], F32)
+        make_identity(nc, ident[:])
+
+        warm = const.tile([P, 1], F32)
+        nc.vector.memset(warm[:], 0.0)
+        nc.scalar.activation(warm[:], warm[:], ACT.Exp)
+
+        ratio_codes = const.tile([P, PASSES, T], U32, align_bytes=64)
+        ratio_scales = const.tile([P, PASSES, T], U8, align_bytes=64)
+        gain_raw = const.tile([P, TILES], BF16)
+        gain = const.tile([P, TILES], F32)
+        prior_raw = const.tile([P, 4], BF16)
+        prior_col = const.tile([P, 4], F32)
+        prior = const.tile([P, T], F32)
+
+        uni_raw, bi_raw, gum_raw, r_raw, r_grp = {}, {}, {}, {}, {}
+        packed, xt, grouped, codes, scales, acc, lw, w_pair, k_pair = {}, {}, {}, {}, {}, {}, {}, {}, {}
+
+        def load_small():
+            nc.scalar.dma_start(out=gain_raw[:], in_=length_gain.rearrange("(p n) -> p n", n=TILES))
+            nc.scalar.dma_start(out=prior_raw[:], in_=log_prior.rearrange("(p c) -> p c", c=4))
+
+        def prep_small():
+            nc.vector.tensor_copy(out=gain[:], in_=gain_raw[:])
+            nc.vector.tensor_copy(out=prior_col[:], in_=prior_raw[:])
+
+        def prior_pe():
+            pt = psum_x.tile([P, 4, P], F32, tag="xt")
+            for c in range(4):
+                nc.tensor.transpose(pt[:, c, :], prior_col[:, c : c + 1].to_broadcast([P, P]), ident[:])
+            nc.vector.tensor_copy(
+                out=prior[:].rearrange("p (q c) -> p q c", c=4), in_=pt[:].rearrange("p c q -> p q c")
+            )
+
+        def load_uni(m):
+            t = raw.tile([P, 2, U], BF16, tag="uni_raw", bufs=6)
+            nc.sync.dma_start(out=t[:], in_=uni_v[:, 2 * m : 2 * m + 2, :])
+            uni_raw[m] = t
+
+        def load_bi(i):
+            t = raw.tile([P, V], BF16, tag="bi_raw", bufs=10)
+            nc.sync.dma_start(out=t[:], in_=bi_v[:, i, :])
+            bi_raw[i] = t
+
+        def load_gumbel(q):
+            t = raw.tile([P, 4, T], BF16, tag="gum", bufs=4)
+            nc.sync.dma_start(out=t[:], in_=gumbel_v[:, 4 * q : 4 * q + 4, :])
+            gum_raw[q] = t
+
+        def load_ratio(c):
+            t = raw.tile([P, 4, T], BF16, tag="r_raw", bufs=4)
+            src = uni_ratio_v[c] if c < UNI_PASSES else bi_ratio_v[c - UNI_PASSES]
+            nc.sync.dma_start(out=t[:], in_=src)
+            r_raw[c] = t
+
+        def interleave(c, lo, hi, engine):
+            if c not in r_grp:
+                g = work.tile([P, T, 4], BF16, tag="r_grp", align_bytes=64)
+                r_grp[c] = g
+            dst = r_grp[c][:, lo:hi, :]
+            src = r_raw[c][:, :, lo:hi].rearrange("p t w -> p w t")
+            if engine == "V":
+                nc.vector.tensor_copy(out=dst, in_=src)
+            else:
+                nc.scalar.copy(out=dst, in_=src)
+
+        def quant_ratio(c):
+            nc.vector.quantize_mx(
+                out=ratio_codes[:, c, :].bitcast(E4M3),
+                scales=ratio_scales[:, c, :],
+                in_=r_grp[c][:].rearrange("p w t -> p (w t)"),
+            )
+
+        def words(i, g):
+            if g < UNI_PASSES:
+                return uni_raw[i // 2][:, i % 2, g * K_PASS : (g + 1) * K_PASS].bitcast(F32)
+            return bi_raw[i][:, (g - UNI_PASSES) * K_PASS : (g - UNI_PASSES + 1) * K_PASS].bitcast(F32)
+
+        def pack(i, lo, hi, engine):
+            if i not in packed:
+                t = work.tile([P, PASSES, 2, P], F32, tag="packed")
+                packed[i] = t
+            if hi <= UNI_PASSES:
+                src = uni_raw[i // 2][:, i % 2, lo * K_PASS : hi * K_PASS]
+            else:
+                src = bi_raw[i][:, (lo - UNI_PASSES) * K_PASS : (hi - UNI_PASSES) * K_PASS]
+            src = src.bitcast(F32).rearrange("p (g w u) -> p g u w", g=hi - lo, u=2)
+            if engine == "S":
+                nc.scalar.copy(out=packed[i][:, lo:hi, :, :], in_=src)
+            else:
+                nc.vector.tensor_copy(out=packed[i][:, lo:hi, :, :], in_=src)
+
+        def transposes(i, b):
+            x = psum_x.tile([P, 2, 2, P], F32, tag="xt")
+            xt[i, b] = x
+            for g in range(2):
+                for u in range(2):
+                    if i in packed:
+                        src = packed[i][:, 2 * b + g, u, :]
+                    else:
+                        src = words(i, 2 * b + g)[:, u : 2 * P : 2]
+                    nc.tensor.transpose(x[:, g, u, :], src, ident[:])
+
+        def evac(i, b, engine="S"):
+            if i not in grouped:
+                t = work.tile([P, PASSES, 4 * P], BF16, tag="grouped", align_bytes=64, bufs=4)
+                grouped[i] = t
+            dst = grouped[i][:, 2 * b : 2 * b + 2, :].bitcast(F32).rearrange("p g (r u) -> p g r u", u=2)
+            src = xt[i, b][:].rearrange("p g u r -> p g r u")
+            if engine == "S":
+                nc.scalar.copy(out=dst, in_=src)
+            else:
+                nc.vector.tensor_copy(out=dst, in_=src)
+
+        def quant_counts(i, lo, hi):
+            if i not in codes:
+                c = work.tile([P, PASSES, P], U32, tag="codes", align_bytes=64, bufs=4)
+                s = work.tile([P, PASSES, P], U8, tag="scales", align_bytes=64, bufs=4)
+                codes[i], scales[i] = c, s
+            nc.vector.quantize_mx(
+                out=codes[i][:, lo:hi, :].rearrange("p g r -> p (g r)").bitcast(E4M3 if hi <= UNI_PASSES else E5M2),
+                scales=scales[i][:, lo:hi, :].rearrange("p g r -> p (g r)"),
+                in_=grouped[i][:, lo:hi, :].rearrange("p g c -> p (g c)"),
+            )
+
+        def quant_uni(i):
+            quant_counts(i, 0, UNI_PASSES)
+
+        def quant_bi(i):
+            quant_counts(i, UNI_PASSES, PASSES)
+
+        def product(i, c):
+            if i not in acc:
+                a = psum_a.tile([P, T], F32, tag="acc")
+                acc[i] = a
+            nc.tensor.matmul_mx(
+                out=acc[i][:],
+                lhsT=codes[i][:, c, :].bitcast(E4M3 if c < UNI_PASSES else E5M2),
+                lhsT_scale=scales[i][:, c, :],
+                rhs=ratio_codes[:, c, :].bitcast(E4M3),
+                rhs_scale=ratio_scales[:, c, :],
+                start=(c == 0),
+                stop=(c == PASSES - 1),
+            )
+
+        def products(i):
+            for c in range(PASSES):
+                product(i, c)
+
+        def log_weight(i):
+            t = outs.tile([P, T], F32, tag="lw")
+            lw[i] = t
+            nc.vector.scalar_tensor_tensor(
+                out=t[:], in0=acc[i][:], scalar=gain[:, i : i + 1], in1=prior[:], op0=MULT, op1=ADD
+            )
+
+        def weight_exp(i):
+            if i % 2 == 0:
+                t = outs.tile([P, 2, T], F32, tag="w_pair")
+                w_pair[i // 2] = t
+            nc.scalar.activation(w_pair[i // 2][:, i % 2, :], lw[i][:], ACT.Exp)
+
+        def key_add(i):
+            if i % 2 == 0:
+                t = outs.tile([P, 2, T], F32, tag="k_pair")
+                k_pair[i // 2] = t
+            nc.vector.tensor_tensor(
+                out=k_pair[i // 2][:, i % 2, :], in0=lw[i][:], in1=gum_raw[i // 4][:, i % 4, :], op=ADD
+            )
+
+        def store(i):
+            m = i // 2
+            if m < TILES // 2 - 1:
+                if i % 2 == 1:
+                    nc.sync.dma_start(out=weight_v[:, 2 * m : 2 * m + 2, :], in_=w_pair[m][:])
+                    nc.sync.dma_start(out=key_v[:, 2 * m : 2 * m + 2, :], in_=k_pair[m][:])
+            else:
+                nc.sync.dma_start(out=weight_v[:, i, :], in_=w_pair[m][:, i % 2, :])
+                nc.sync.dma_start(out=key_v[:, i, :], in_=k_pair[m][:, i % 2, :])
+
+        load_small()
+        load_ratio(0)
+        load_uni(0)
+        load_ratio(1)
+        load_bi(0)
+        load_ratio(2)
+        load_ratio(3)
+        load_bi(1)
+        load_ratio(4)
+        load_uni(1)
+        load_ratio(5)
+        load_bi(2)
+        load_bi(3)
+        load_uni(2)
+        load_bi(4)
+        load_bi(5)
+        load_gumbel(0)
+        load_uni(3)
+        load_bi(6)
+        load_bi(7)
+        interleave(0, 0, 176, "S")
+        interleave(0, 176, 512, "V")
+        transposes(0, 0)
+        transposes(1, 0)
+        prep_small()
+        quant_ratio(0)
+        evac(0, 0)
+        evac(1, 0)
+        interleave(1, 0, 112, "S")
+        interleave(1, 112, 512, "V")
+        quant_uni(0)
+        quant_uni(1)
+        quant_ratio(1)
+        transposes(0, 1)
+        transposes(0, 2)
+        product(0, 0)
+        product(1, 0)
+        product(0, 1)
+        product(1, 1)
+        evac(0, 1)
+        evac(0, 2)
+        interleave(2, 0, 128, "S")
+        interleave(2, 128, 512, "V")
+        quant_bi(0)
+        quant_ratio(2)
+        interleave(3, 0, 192, "S")
+        interleave(3, 192, 512, "V")
+        transposes(1, 1)
+        transposes(1, 2)
+        quant_ratio(3)
+        evac(1, 1)
+        evac(1, 2)
+        prior_pe()
+        quant_bi(1)
+        transposes(2, 0)
+        transposes(3, 0)
+        for c in (2, 3):
+            product(0, c)
+            product(1, c)
+        interleave(4, 0, 128, "S")
+        interleave(4, 128, 512, "V")
+        evac(2, 0)
+        evac(3, 0)
+        quant_ratio(4)
+        quant_uni(2)
+        quant_uni(3)
+        interleave(5, 0, 192, "S")
+        interleave(5, 192, 512, "V")
+        transposes(2, 1)
+        transposes(2, 2)
+        quant_ratio(5)
+        for c in (4, 5):
+            product(0, c)
+            product(1, c)
+        transposes(3, 1)
+        transposes(3, 2)
+        for b in (1, 2):
+            evac(2, b)
+        for b in (1, 2):
+            evac(3, b)
+        pack(4, 0, 2, "S")
+        pack(4, 2, 6, "V")
+        quant_bi(2)
+        pack(5, 0, 2, "V")
+        pack(5, 2, 6, "V")
+        quant_bi(3)
+        for m in range(2, TILES // 2 + 2):
+            i, j = 2 * m, 2 * m + 1
+            if i < TILES:
+                for t in (i, j):
+                    for b in range(3):
+                        transposes(t, b)
+            if i - 2 < TILES:
+                products(i - 2)
+                products(j - 2)
+            if j + 4 < TILES:
+                load_uni(m + 2)
+                load_bi(i + 4)
+                load_bi(j + 4)
+            if m % 2 == 0 and m < TILES // 2:
+                load_gumbel(m // 2)
+            log_weight(i - 4)
+            if i < TILES:
+                for b in range(3):
+                    evac(i, b)
+            weight_exp(i - 4)
+            log_weight(j - 4)
+            if j + 2 < TILES:
+                pack(i + 2, 0, 2, "S")
+                pack(i + 2, 2, 6, "V")
+            if i < TILES:
+                for b in range(3):
+                    evac(j, b)
+            weight_exp(j - 4)
+            key_add(i - 4)
+            if i < TILES:
+                quant_uni(i)
+                quant_bi(i)
+            if j + 2 < TILES:
+                pack(j + 2, 0, 2, "V")
+                pack(j + 2, 2, 6, "V")
+            key_add(j - 4)
+            if i < TILES:
+                quant_uni(j)
+                quant_bi(j)
+            store(i - 4)
+            store(j - 4)

@@ -42,8 +42,8 @@ def tile_dsir_importance_weights_s2_kernel(
         raw = ctx.enter_context(tc.tile_pool(name="raw", bufs=1))
         work = ctx.enter_context(tc.tile_pool(name="work", bufs=3))
         outs = ctx.enter_context(tc.tile_pool(name="outs", bufs=3))
-        psum_x = ctx.enter_context(tc.psum_pool(name="psum_x", bufs=6))
-        psum_a = ctx.enter_context(tc.psum_pool(name="psum_a", bufs=2))
+        psum_x = ctx.enter_context(tc.psum_pool(name="psum_x", bufs=5))
+        psum_a = ctx.enter_context(tc.psum_pool(name="psum_a", bufs=3))
         ctx.enter_context(tc.manual_schedule())
 
         ident = const.tile([P, P], F32)
@@ -218,7 +218,7 @@ def tile_dsir_importance_weights_s2_kernel(
 
         def store(i):
             m = i // 2
-            if m < TILES // 2 - 1:
+            if m < TILES // 2 - 2:
                 if i % 2 == 1:
                     nc.sync.dma_start(out=weight_v[:, 2 * m : 2 * m + 2, :], in_=w_pair[m][:])
                     nc.sync.dma_start(out=key_v[:, 2 * m : 2 * m + 2, :], in_=k_pair[m][:])
@@ -246,6 +246,10 @@ def tile_dsir_importance_weights_s2_kernel(
         load_uni(3)
         load_bi(6)
         load_bi(7)
+        load_gumbel(1)
+        load_uni(4)
+        load_bi(8)
+        load_bi(9)
         interleave(0, 0, 176, "S")
         interleave(0, 176, 512, "V")
         transposes(0, 0)
@@ -254,21 +258,21 @@ def tile_dsir_importance_weights_s2_kernel(
         quant_ratio(0)
         evac(0, 0)
         evac(1, 0)
-        interleave(1, 0, 112, "S")
-        interleave(1, 112, 512, "V")
+        interleave(1, 0, 160, "S")
+        interleave(1, 160, 512, "V")
         quant_uni(0)
         quant_uni(1)
         quant_ratio(1)
         transposes(0, 1)
         transposes(0, 2)
+        evac(0, 1)
+        evac(0, 2)
         product(0, 0)
         product(1, 0)
         product(0, 1)
         product(1, 1)
-        evac(0, 1)
-        evac(0, 2)
-        interleave(2, 0, 128, "S")
-        interleave(2, 128, 512, "V")
+        interleave(2, 0, 160, "S")
+        interleave(2, 160, 512, "V")
         quant_bi(0)
         quant_ratio(2)
         interleave(3, 0, 192, "S")
@@ -278,78 +282,70 @@ def tile_dsir_importance_weights_s2_kernel(
         quant_ratio(3)
         evac(1, 1)
         evac(1, 2)
-        prior_pe()
+        interleave(4, 0, 192, "S")
+        interleave(4, 192, 512, "V")
         quant_bi(1)
         transposes(2, 0)
         transposes(3, 0)
-        for c in (2, 3):
-            product(0, c)
-            product(1, c)
-        interleave(4, 0, 128, "S")
-        interleave(4, 128, 512, "V")
+        for c in (2, 3): product(0, c); product(1, c)
+        quant_ratio(4)
         evac(2, 0)
         evac(3, 0)
-        quant_ratio(4)
-        quant_uni(2)
-        quant_uni(3)
         interleave(5, 0, 192, "S")
         interleave(5, 192, 512, "V")
+        quant_uni(2)
+        quant_ratio(5)
+        quant_uni(3)
         transposes(2, 1)
         transposes(2, 2)
-        quant_ratio(5)
-        for c in (4, 5):
-            product(0, c)
-            product(1, c)
+        for c in (4, 5): product(0, c); product(1, c)
+        evac(2, 1)
+        evac(2, 2)
         transposes(3, 1)
         transposes(3, 2)
-        for b in (1, 2):
-            evac(2, b)
-        for b in (1, 2):
-            evac(3, b)
+        quant_bi(2)
+        prior_pe()
+        products(2)
+        log_weight(0)
+        evac(3, 1)
+        evac(3, 2)
+        weight_exp(0)
         pack(4, 0, 2, "S")
         pack(4, 2, 6, "V")
-        quant_bi(2)
-        pack(5, 0, 2, "V")
-        pack(5, 2, 6, "V")
         quant_bi(3)
-        for m in range(2, TILES // 2 + 2):
-            i, j = 2 * m, 2 * m + 1
-            if i < TILES:
-                for t in (i, j):
-                    for b in range(3):
-                        transposes(t, b)
-            if i - 2 < TILES:
-                products(i - 2)
-                products(j - 2)
-            if j + 4 < TILES:
-                load_uni(m + 2)
-                load_bi(i + 4)
-                load_bi(j + 4)
-            if m % 2 == 0 and m < TILES // 2:
-                load_gumbel(m // 2)
-            log_weight(i - 4)
-            if i < TILES:
+        key_add(0)
+        log_weight(1)
+        weight_exp(1)
+        key_add(1)
+        store(0)
+        store(1)
+        for s in range(4, TILES + 2):
+            if s < TILES:
                 for b in range(3):
-                    evac(i, b)
-            weight_exp(i - 4)
-            log_weight(j - 4)
-            if j + 2 < TILES:
-                pack(i + 2, 0, 2, "S")
-                pack(i + 2, 2, 6, "V")
-            if i < TILES:
-                for b in range(3):
-                    evac(j, b)
-            weight_exp(j - 4)
-            key_add(i - 4)
-            if i < TILES:
-                quant_uni(i)
-                quant_bi(i)
-            if j + 2 < TILES:
-                pack(j + 2, 0, 2, "V")
-                pack(j + 2, 2, 6, "V")
-            key_add(j - 4)
-            if i < TILES:
-                quant_uni(j)
-                quant_bi(j)
-            store(i - 4)
-            store(j - 4)
+                    transposes(s, b)
+            if s - 1 < TILES:
+                products(s - 1)
+            if s + 6 < TILES:
+                if s % 2 == 0:
+                    load_uni((s + 6) // 2)
+                load_bi(s + 6)
+            if s % 4 == 0 and s + 4 < TILES:
+                load_gumbel(s // 4 + 1)
+            log_weight(s - 2)
+            if s < TILES:
+                evac(s, 0)
+                evac(s, 1)
+                evac(s, 2)
+            if s == 4:
+                pack(5, 0, 2, "V")
+                pack(5, 2, 6, "V")
+            if s < TILES:
+                quant_uni(s)
+            weight_exp(s - 2)
+            key_add(s - 2)
+            if s < TILES:
+                quant_bi(s)
+            if s + 2 < TILES:
+                pack(s + 2, 0, 2, "S" if s % 2 == 0 else "V")
+                pack(s + 2, 2, 6, "V")
+            store(s - 2)

@@ -22,7 +22,8 @@ UNI_PASSES = U // K_PASS
 BI_PASSES = V // K_PASS
 PASSES = UNI_PASSES + BI_PASSES
 TILES = D // P
-HALF = T // 2
+KEYS = {4: (0, 1), 14: (11, 12), 15: (13,), 16: (14,), 17: (15,)}
+STORES = ((0, 2), (2, 4), (4, 6), (6, 8), (8, 10), (10, 12), (12, 13), (13, 14), (14, 15), (15, 16))
 
 
 def tile_dsir_importance_weights_s2_kernel(
@@ -80,20 +81,23 @@ def tile_dsir_importance_weights_s2_kernel(
                 out=prior[:].rearrange("p (q c) -> p q c", c=4), in_=pt[:].rearrange("p c q -> p q c")
             )
 
-        def load_uni(m):
-            t = raw.tile([P, 2, U], BF16, tag="uni_raw", bufs=6)
-            nc.sync.dma_start(out=t[:], in_=uni_v[:, 2 * m : 2 * m + 2, :])
-            uni_raw[m] = t
+        def load_uni(lo, hi):
+            if lo % 4 == 0:
+                t = raw.tile([P, 4, U], BF16, tag="uni_raw", bufs=3)
+                uni_raw[lo // 4] = t
+            nc.sync.dma_start(out=uni_raw[lo // 4][:, lo % 4 : lo % 4 + hi - lo, :], in_=uni_v[:, lo:hi, :])
 
-        def load_bi(i):
-            t = raw.tile([P, V], BF16, tag="bi_raw", bufs=10)
-            nc.sync.dma_start(out=t[:], in_=bi_v[:, i, :])
-            bi_raw[i] = t
+        def load_bi(lo, hi):
+            if lo % 2 == 0:
+                t = raw.tile([P, 2, V], BF16, tag="bi_raw", bufs=6)
+                bi_raw[lo // 2] = t
+            nc.sync.dma_start(out=bi_raw[lo // 2][:, lo % 2 : lo % 2 + hi - lo, :], in_=bi_v[:, lo:hi, :])
 
-        def load_gumbel(q):
-            t = raw.tile([P, 4, T], BF16, tag="gum", bufs=4)
-            nc.sync.dma_start(out=t[:], in_=gumbel_v[:, 4 * q : 4 * q + 4, :])
-            gum_raw[q] = t
+        def load_gumbel(lo, hi):
+            if lo % 8 == 0:
+                t = raw.tile([P, 8, T], BF16, tag="gum", bufs=2)
+                gum_raw[lo // 8] = t
+            nc.sync.dma_start(out=gum_raw[lo // 8][:, lo % 8 : lo % 8 + hi - lo, :], in_=gumbel_v[:, lo:hi, :])
 
         def load_ratio(c):
             t = raw.tile([P, 4, T], BF16, tag="r_raw", bufs=4)
@@ -121,17 +125,17 @@ def tile_dsir_importance_weights_s2_kernel(
 
         def words(i, g):
             if g < UNI_PASSES:
-                return uni_raw[i // 2][:, i % 2, g * K_PASS : (g + 1) * K_PASS].bitcast(F32)
-            return bi_raw[i][:, (g - UNI_PASSES) * K_PASS : (g - UNI_PASSES + 1) * K_PASS].bitcast(F32)
+                return uni_raw[i // 4][:, i % 4, g * K_PASS : (g + 1) * K_PASS].bitcast(F32)
+            return bi_raw[i // 2][:, i % 2, (g - UNI_PASSES) * K_PASS : (g - UNI_PASSES + 1) * K_PASS].bitcast(F32)
 
         def pack(i, lo, hi, engine):
             if i not in packed:
                 t = work.tile([P, PASSES, 2, P], F32, tag="packed")
                 packed[i] = t
             if hi <= UNI_PASSES:
-                src = uni_raw[i // 2][:, i % 2, lo * K_PASS : hi * K_PASS]
+                src = uni_raw[i // 4][:, i % 4, lo * K_PASS : hi * K_PASS]
             else:
-                src = bi_raw[i][:, (lo - UNI_PASSES) * K_PASS : (hi - UNI_PASSES) * K_PASS]
+                src = bi_raw[i // 2][:, i % 2, (lo - UNI_PASSES) * K_PASS : (hi - UNI_PASSES) * K_PASS]
             src = src.bitcast(F32).rearrange("p (g w u) -> p g u w", g=hi - lo, u=2)
             if engine == "S":
                 nc.scalar.copy(out=packed[i][:, lo:hi, :, :], in_=src)
@@ -196,7 +200,7 @@ def tile_dsir_importance_weights_s2_kernel(
                 product(i, c)
 
         def log_weight(i):
-            t = outs.tile([P, T], F32, tag="lw")
+            t = outs.tile([P, T], F32, tag="lw", bufs=5)
             lw[i] = t
             nc.vector.scalar_tensor_tensor(
                 out=t[:], in0=acc[i][:], scalar=gain[:, i : i + 1], in1=prior[:], op0=MULT, op1=ADD
@@ -204,148 +208,146 @@ def tile_dsir_importance_weights_s2_kernel(
 
         def weight_exp(i):
             if i % 2 == 0:
-                t = outs.tile([P, 2, T], F32, tag="w_pair")
+                t = outs.tile([P, 2, T], F32, tag="w_out", bufs=4)
                 w_pair[i // 2] = t
             nc.scalar.activation(w_pair[i // 2][:, i % 2, :], lw[i][:], ACT.Exp)
 
         def key_add(i):
             if i % 2 == 0:
-                t = outs.tile([P, 2, T], F32, tag="k_pair")
+                t = outs.tile([P, 2, T], F32, tag="k_out", bufs=3)
                 k_pair[i // 2] = t
             nc.vector.tensor_tensor(
-                out=k_pair[i // 2][:, i % 2, :], in0=lw[i][:], in1=gum_raw[i // 4][:, i % 4, :], op=ADD
+                out=k_pair[i // 2][:, i % 2, :], in0=lw[i][:], in1=gum_raw[i // 8][:, i % 8, :], op=ADD
             )
 
         def store(i):
-            m = i // 2
-            if m < TILES // 2 - 2:
-                if i % 2 == 1:
-                    nc.sync.dma_start(out=weight_v[:, 2 * m : 2 * m + 2, :], in_=w_pair[m][:])
-                    nc.sync.dma_start(out=key_v[:, 2 * m : 2 * m + 2, :], in_=k_pair[m][:])
-            else:
-                nc.sync.dma_start(out=weight_v[:, i, :], in_=w_pair[m][:, i % 2, :])
-                nc.sync.dma_start(out=key_v[:, i, :], in_=k_pair[m][:, i % 2, :])
+            for lo, hi in STORES:
+                if hi == i + 1:
+                    a, b = lo % 2, lo % 2 + hi - lo
+                    nc.sync.dma_start(out=weight_v[:, lo:hi, :], in_=w_pair[i // 2][:, a:b, :])
+                    nc.sync.dma_start(out=key_v[:, lo:hi, :], in_=k_pair[i // 2][:, a:b, :])
 
         load_small()
+        load_uni(0, 2)
         load_ratio(0)
-        load_uni(0)
         load_ratio(1)
-        load_bi(0)
+        load_bi(0, 1)
         load_ratio(2)
         load_ratio(3)
-        load_bi(1)
+        load_bi(1, 2)
+        load_uni(2, 4)
         load_ratio(4)
-        load_uni(1)
+        load_bi(2, 4)
         load_ratio(5)
-        load_bi(2)
-        load_bi(3)
-        load_uni(2)
-        load_bi(4)
-        load_bi(5)
-        load_gumbel(0)
-        load_uni(3)
-        load_bi(6)
-        load_bi(7)
-        load_gumbel(1)
-        load_uni(4)
-        load_bi(8)
-        load_bi(9)
-        interleave(0, 0, 176, "S")
-        interleave(0, 176, 512, "V")
+        load_uni(4, 6)
+        load_bi(4, 6)
+        load_uni(6, 8)
+        load_gumbel(0, 4)
+        load_bi(6, 8)
+        load_bi(8, 10)
+        load_gumbel(4, 8)
+        load_uni(8, 12)
+        prep_small()
+        prior_pe()
         transposes(0, 0)
         transposes(1, 0)
-        prep_small()
-        quant_ratio(0)
         evac(0, 0)
+        interleave(0, 0, 320, "S")
+        interleave(0, 320, 512, "V")
         evac(1, 0)
-        interleave(1, 0, 160, "S")
-        interleave(1, 160, 512, "V")
         quant_uni(0)
+        interleave(1, 0, 144, "S")
+        interleave(1, 144, 512, "V")
         quant_uni(1)
+        quant_ratio(0)
         quant_ratio(1)
         transposes(0, 1)
         transposes(0, 2)
-        evac(0, 1)
-        evac(0, 2)
         product(0, 0)
-        product(1, 0)
         product(0, 1)
+        product(1, 0)
         product(1, 1)
-        interleave(2, 0, 160, "S")
-        interleave(2, 160, 512, "V")
-        quant_bi(0)
-        quant_ratio(2)
-        interleave(3, 0, 192, "S")
-        interleave(3, 192, 512, "V")
+        evac(0, 1)
+        interleave(2, 0, 64, "S")
+        interleave(2, 64, 512, "V")
+        evac(0, 2)
+        interleave(3, 0, 32, "S")
+        interleave(3, 32, 512, "V")
         transposes(1, 1)
         transposes(1, 2)
-        quant_ratio(3)
+        quant_bi(0)
+        quant_ratio(2)
         evac(1, 1)
         evac(1, 2)
-        interleave(4, 0, 192, "S")
-        interleave(4, 192, 512, "V")
-        quant_bi(1)
         transposes(2, 0)
         transposes(3, 0)
-        for c in (2, 3): product(0, c); product(1, c)
-        quant_ratio(4)
+        quant_ratio(3)
         evac(2, 0)
+        quant_bi(1)
+        interleave(4, 0, 112, "S")
+        interleave(4, 112, 512, "V")
+        product(0, 2)
+        product(0, 3)
+        product(1, 2)
+        product(1, 3)
         evac(3, 0)
-        interleave(5, 0, 192, "S")
-        interleave(5, 192, 512, "V")
         quant_uni(2)
-        quant_ratio(5)
         quant_uni(3)
+        quant_ratio(4)
+        product(2, 0)
+        product(2, 1)
         transposes(2, 1)
         transposes(2, 2)
-        for c in (4, 5): product(0, c); product(1, c)
-        evac(2, 1)
-        evac(2, 2)
         transposes(3, 1)
         transposes(3, 2)
+        evac(2, 1)
+        interleave(5, 0, 128, "S")
+        interleave(5, 128, 512, "V")
+        evac(2, 2)
+        quant_ratio(5)
+        product(0, 4)
+        product(1, 4)
+        product(0, 5)
+        product(1, 5)
         quant_bi(2)
-        prior_pe()
-        products(2)
-        log_weight(0)
         evac(3, 1)
         evac(3, 2)
-        weight_exp(0)
+        product(2, 2)
+        product(2, 3)
+        product(2, 4)
+        product(2, 5)
+        log_weight(0)
         pack(4, 0, 2, "S")
         pack(4, 2, 6, "V")
         quant_bi(3)
-        key_add(0)
+        pack(5, 0, 2, "V")
+        pack(5, 2, 6, "V")
         log_weight(1)
-        weight_exp(1)
-        key_add(1)
-        store(0)
-        store(1)
         for s in range(4, TILES + 2):
             if s < TILES:
                 for b in range(3):
                     transposes(s, b)
             if s - 1 < TILES:
                 products(s - 1)
-            if s + 6 < TILES:
-                if s % 2 == 0:
-                    load_uni((s + 6) // 2)
-                load_bi(s + 6)
-            if s % 4 == 0 and s + 4 < TILES:
-                load_gumbel(s // 4 + 1)
+            if s % 2 == 0 and s + 6 < TILES:
+                load_bi(s + 6, s + 8)
+            if s % 4 == 0 and s + 8 < TILES:
+                load_uni(s + 8, s + 12)
+            if s == 6:
+                load_gumbel(8, 16)
             log_weight(s - 2)
             if s < TILES:
                 evac(s, 0)
                 evac(s, 1)
                 evac(s, 2)
-            if s == 4:
-                pack(5, 0, 2, "V")
-                pack(5, 2, 6, "V")
-            if s < TILES:
                 quant_uni(s)
-            weight_exp(s - 2)
-            key_add(s - 2)
+            for i in KEYS.get(s, (s - 3,)):
+                weight_exp(i)
+                key_add(i)
             if s < TILES:
                 quant_bi(s)
             if s + 2 < TILES:
                 pack(s + 2, 0, 2, "S" if s % 2 == 0 else "V")
                 pack(s + 2, 2, 6, "V")
-            store(s - 2)
+            for i in KEYS.get(s, (s - 3,)):
+                store(i)

@@ -22,7 +22,7 @@ UNI_PASSES = U // K_PASS
 BI_PASSES = V // K_PASS
 PASSES = UNI_PASSES + BI_PASSES
 TILES = D // P
-KEYS = {4: (0, 1), 14: (11, 12), 15: (13,), 16: (14,), 17: (15,)}
+KEYS = {**{s: (s - 3,) for s in range(5, 7)}, **{s: (s - 2,) for s in range(8, 18)}, 4: (0, 1), 7: (4, 5)}
 STORES = ((0, 2), (2, 4), (4, 6), (6, 8), (8, 10), (10, 12), (12, 13), (13, 14), (14, 15), (15, 16))
 
 
@@ -50,10 +50,6 @@ def tile_dsir_importance_weights_s2_kernel(
         ident = const.tile([P, P], F32)
         make_identity(nc, ident[:])
 
-        warm = const.tile([P, 1], F32)
-        nc.vector.memset(warm[:], 0.0)
-        nc.scalar.activation(warm[:], warm[:], ACT.Exp)
-
         ratio_codes = const.tile([P, PASSES, T], U32, align_bytes=64)
         ratio_scales = const.tile([P, PASSES, T], U8, align_bytes=64)
         gain_raw = const.tile([P, TILES], BF16)
@@ -65,9 +61,17 @@ def tile_dsir_importance_weights_s2_kernel(
         uni_raw, bi_raw, gum_raw, r_raw, r_grp = {}, {}, {}, {}, {}
         packed, xt, grouped, codes, scales, acc, lw, w_pair, k_pair = {}, {}, {}, {}, {}, {}, {}, {}, {}
 
+        def parts(i):
+            return ((0, T),) if i < TILES - 1 else ((0, T // 2), (T // 2, T))
+
         def load_small():
             nc.scalar.dma_start(out=gain_raw[:], in_=length_gain.rearrange("(p n) -> p n", n=TILES))
             nc.scalar.dma_start(out=prior_raw[:], in_=log_prior.rearrange("(p c) -> p c", c=4))
+
+        def warm_exp():
+            warm = const.tile([P, 1], F32)
+            nc.vector.memset(warm[:], 0.0)
+            nc.scalar.activation(warm[:], warm[:], ACT.Exp)
 
         def prep_small():
             nc.vector.tensor_copy(out=gain[:], in_=gain_raw[:])
@@ -75,10 +79,13 @@ def tile_dsir_importance_weights_s2_kernel(
 
         def prior_pe():
             pt = psum_x.tile([P, 4, P], F32, tag="xt")
+            xt["prior"] = pt
             for c in range(4):
                 nc.tensor.transpose(pt[:, c, :], prior_col[:, c : c + 1].to_broadcast([P, P]), ident[:])
+
+        def prior_out():
             nc.vector.tensor_copy(
-                out=prior[:].rearrange("p (q c) -> p q c", c=4), in_=pt[:].rearrange("p c q -> p q c")
+                out=prior[:].rearrange("p (q c) -> p q c", c=4), in_=xt["prior"][:].rearrange("p c q -> p q c")
             )
 
         def load_uni(lo, hi):
@@ -89,7 +96,7 @@ def tile_dsir_importance_weights_s2_kernel(
 
         def load_bi(lo, hi):
             if lo % 2 == 0:
-                t = raw.tile([P, 2, V], BF16, tag="bi_raw", bufs=6)
+                t = raw.tile([P, 2, V], BF16, tag="bi_raw", bufs=5)
                 bi_raw[lo // 2] = t
             nc.sync.dma_start(out=bi_raw[lo // 2][:, lo % 2 : lo % 2 + hi - lo, :], in_=bi_v[:, lo:hi, :])
 
@@ -202,19 +209,21 @@ def tile_dsir_importance_weights_s2_kernel(
         def log_weight(i):
             t = outs.tile([P, T], F32, tag="lw", bufs=5)
             lw[i] = t
-            nc.vector.scalar_tensor_tensor(
-                out=t[:], in0=acc[i][:], scalar=gain[:, i : i + 1], in1=prior[:], op0=MULT, op1=ADD
-            )
+            for lo, hi in parts(i):
+                nc.vector.scalar_tensor_tensor(
+                    out=t[:, lo:hi], in0=acc[i][:, lo:hi], scalar=gain[:, i : i + 1], in1=prior[:, lo:hi], op0=MULT, op1=ADD
+                )
 
         def weight_exp(i):
             if i % 2 == 0:
                 t = outs.tile([P, 2, T], F32, tag="w_out", bufs=4)
                 w_pair[i // 2] = t
-            nc.scalar.activation(w_pair[i // 2][:, i % 2, :], lw[i][:], ACT.Exp)
+            for lo, hi in parts(i):
+                nc.scalar.activation(w_pair[i // 2][:, i % 2, lo:hi], lw[i][:, lo:hi], ACT.Exp)
 
         def key_add(i):
             if i % 2 == 0:
-                t = outs.tile([P, 2, T], F32, tag="k_out", bufs=3)
+                t = outs.tile([P, 2, T], F32, tag="k_out", bufs=4)
                 k_pair[i // 2] = t
             nc.vector.tensor_tensor(
                 out=k_pair[i // 2][:, i % 2, :], in0=lw[i][:], in1=gum_raw[i // 8][:, i % 8, :], op=ADD
@@ -230,98 +239,101 @@ def tile_dsir_importance_weights_s2_kernel(
         load_small()
         load_uni(0, 2)
         load_ratio(0)
-        load_ratio(1)
         load_bi(0, 1)
-        load_ratio(2)
-        load_ratio(3)
+        load_ratio(1)
         load_bi(1, 2)
         load_uni(2, 4)
+        load_ratio(2)
+        load_ratio(3)
         load_ratio(4)
-        load_bi(2, 4)
+        load_bi(2, 3)
         load_ratio(5)
+        load_bi(3, 4)
         load_uni(4, 6)
         load_bi(4, 6)
-        load_uni(6, 8)
-        load_gumbel(0, 4)
         load_bi(6, 8)
+        load_gumbel(0, 4)
+        load_uni(6, 8)
         load_bi(8, 10)
-        load_gumbel(4, 8)
         load_uni(8, 12)
-        prep_small()
-        prior_pe()
+        load_gumbel(4, 8)
+        warm_exp()
         transposes(0, 0)
         transposes(1, 0)
+        transposes(0, 1)
+        transposes(0, 2)
         evac(0, 0)
-        interleave(0, 0, 320, "S")
-        interleave(0, 320, 512, "V")
+        prep_small()
+        transposes(1, 1)
+        transposes(1, 2)
         evac(1, 0)
         quant_uni(0)
-        interleave(1, 0, 144, "S")
-        interleave(1, 144, 512, "V")
+        interleave(0, 0, 304, "S")
+        interleave(0, 304, 512, "V")
+        evac(0, 1)
+        prior_pe()
+        interleave(1, 0, 64, "S")
+        interleave(1, 64, 512, "V")
+        transposes(2, 0)
+        transposes(3, 0)
+        evac(0, 2)
+        evac(1, 1)
         quant_uni(1)
         quant_ratio(0)
         quant_ratio(1)
-        transposes(0, 1)
-        transposes(0, 2)
+        quant_bi(0)
         product(0, 0)
         product(0, 1)
         product(1, 0)
         product(1, 1)
-        evac(0, 1)
-        interleave(2, 0, 64, "S")
-        interleave(2, 64, 512, "V")
-        evac(0, 2)
-        interleave(3, 0, 32, "S")
-        interleave(3, 32, 512, "V")
-        transposes(1, 1)
-        transposes(1, 2)
-        quant_bi(0)
-        quant_ratio(2)
-        evac(1, 1)
         evac(1, 2)
-        transposes(2, 0)
-        transposes(3, 0)
-        quant_ratio(3)
-        evac(2, 0)
+        prior_out()
+        interleave(2, 0, 256, "S")
+        interleave(2, 256, 512, "V")
         quant_bi(1)
-        interleave(4, 0, 112, "S")
-        interleave(4, 112, 512, "V")
-        product(0, 2)
-        product(0, 3)
-        product(1, 2)
-        product(1, 3)
-        evac(3, 0)
+        evac(2, 0)
         quant_uni(2)
+        quant_ratio(2)
+        evac(3, 0)
+        interleave(3, 0, 304, "S")
+        interleave(3, 304, 512, "V")
         quant_uni(3)
-        quant_ratio(4)
-        product(2, 0)
-        product(2, 1)
+        product(0, 2)
+        product(1, 2)
+        quant_ratio(3)
         transposes(2, 1)
         transposes(2, 2)
-        transposes(3, 1)
-        transposes(3, 2)
-        evac(2, 1)
+        interleave(4, 0, 240, "S")
+        interleave(4, 240, 512, "V")
+        evac(2, 2)
+        product(2, 0)
+        product(2, 1)
+        quant_ratio(4)
         interleave(5, 0, 128, "S")
         interleave(5, 128, 512, "V")
-        evac(2, 2)
+        evac(2, 1)
+        product(0, 3)
+        product(1, 3)
+        transposes(3, 1)
+        transposes(3, 2)
+        evac(3, 1)
+        quant_bi(2)
         quant_ratio(5)
         product(0, 4)
         product(1, 4)
-        product(0, 5)
-        product(1, 5)
-        quant_bi(2)
-        evac(3, 1)
-        evac(3, 2)
         product(2, 2)
         product(2, 3)
         product(2, 4)
-        product(2, 5)
-        log_weight(0)
+        evac(3, 2)
         pack(4, 0, 2, "S")
-        pack(4, 2, 6, "V")
+        product(0, 5)
+        product(1, 5)
+        product(2, 5)
         quant_bi(3)
-        pack(5, 0, 2, "V")
+        pack(4, 2, 6, "V")
+        pack(5, 0, 2, "S")
         pack(5, 2, 6, "V")
+        log_weight(0)
         log_weight(1)
         for s in range(4, TILES + 2):
             if s < TILES:
@@ -341,13 +353,13 @@ def tile_dsir_importance_weights_s2_kernel(
                 evac(s, 1)
                 evac(s, 2)
                 quant_uni(s)
-            for i in KEYS.get(s, (s - 3,)):
+            for i in KEYS[s]:
                 weight_exp(i)
                 key_add(i)
             if s < TILES:
                 quant_bi(s)
             if s + 2 < TILES:
-                pack(s + 2, 0, 2, "S" if s % 2 == 0 else "V")
+                pack(s + 2, 0, 2, "S" if s % 4 != 3 else "V")
                 pack(s + 2, 2, 6, "V")
-            for i in KEYS.get(s, (s - 3,)):
+            for i in KEYS[s]:
                 store(i)

from contextlib import ExitStack

import concourse.mybir as mybir
from concourse.masks import make_identity

D, U, V, T = 2048, 1024, 2048, 512
FLOPS = 2 * D * T * (U + V)

F32 = mybir.dt.float32
BF16 = mybir.dt.bfloat16
U32 = mybir.dt.uint32
U8 = mybir.dt.uint8
E4M3 = mybir.dt.float8_e4m3fn_x4
E5M2 = mybir.dt.float8_e5m2_x4
ADD = mybir.AluOpType.add
MULT = mybir.AluOpType.mult
ACT = mybir.ActivationFunctionType

P = 128
K_PASS = 512
UNI_PASSES = U // K_PASS
BI_PASSES = V // K_PASS
PASSES = UNI_PASSES + BI_PASSES
TILES = D // P
KEYS = {**{s: (s - 3,) for s in range(5, 7)}, **{s: (s - 2,) for s in range(8, 18)}, 4: (0, 1), 7: (4, 5)}
STORES = ((0, 2), (2, 4), (4, 6), (6, 8), (8, 10), (10, 12), (12, 13), (13, 14), (14, 15), (15, 16))


def tile_dsir_importance_weights_s2_kernel(
    tc, uni_counts, bi_counts, uni_ratio, bi_ratio, length_gain, log_prior, gumbel, weight, key
):
    nc = tc.nc
    uni_v = uni_counts.rearrange("(p n) k -> p n k", n=TILES)
    bi_v = bi_counts.rearrange("(p n) k -> p n k", n=TILES)
    gumbel_v = gumbel.rearrange("(p n) j -> p n j", n=TILES)
    weight_v = weight.rearrange("(p n) j -> p n j", n=TILES)
    key_v = key.rearrange("(p n) j -> p n j", n=TILES)
    uni_ratio_v = uni_ratio.rearrange("(g p t) j -> g p t j", p=P, t=4)
    bi_ratio_v = bi_ratio.rearrange("(g p t) j -> g p t j", p=P, t=4)

    with ExitStack() as ctx:
        const = ctx.enter_context(tc.tile_pool(name="const", bufs=1))
        raw = ctx.enter_context(tc.tile_pool(name="raw", bufs=1))
        work = ctx.enter_context(tc.tile_pool(name="work", bufs=3))
        outs = ctx.enter_context(tc.tile_pool(name="outs", bufs=3))
        psum_x = ctx.enter_context(tc.psum_pool(name="psum_x", bufs=5))
        psum_a = ctx.enter_context(tc.psum_pool(name="psum_a", bufs=3))
        ctx.enter_context(tc.manual_schedule())

        ident = const.tile([P, P], F32)
        make_identity(nc, ident[:])

        ratio_codes = const.tile([P, PASSES, T], U32, align_bytes=64)
        ratio_scales = const.tile([P, PASSES, T], U8, align_bytes=64)
        gain_raw = const.tile([P, TILES], BF16)
        gain = const.tile([P, TILES], F32)
        prior_raw = const.tile([P, 4], BF16)
        prior_col = const.tile([P, 4], F32)
        prior = const.tile([P, T], F32)

        uni_raw, bi_raw, gum_raw, r_raw, r_grp = {}, {}, {}, {}, {}
        packed, xt, grouped, codes, scales, acc, lw, w_pair, k_pair = {}, {}, {}, {}, {}, {}, {}, {}, {}

        def parts(i):
            return ((0, T),) if i < TILES - 1 else ((0, T // 2), (T // 2, T))

        def load_small():
            nc.scalar.dma_start(out=gain_raw[:], in_=length_gain.rearrange("(p n) -> p n", n=TILES))
            nc.scalar.dma_start(out=prior_raw[:], in_=log_prior.rearrange("(p c) -> p c", c=4))

        def warm_exp():
            warm = const.tile([P, 1], F32)
            nc.vector.memset(warm[:], 0.0)
            nc.scalar.activation(warm[:], warm[:], ACT.Exp)

        def prep_small():
            nc.vector.tensor_copy(out=gain[:], in_=gain_raw[:])
            nc.vector.tensor_copy(out=prior_col[:], in_=prior_raw[:])

        def prior_pe():
            pt = psum_x.tile([P, 4, P], F32, tag="xt")
            xt["prior"] = pt
            for c in range(4):
                nc.tensor.transpose(pt[:, c, :], prior_col[:, c : c + 1].to_broadcast([P, P]), ident[:])

        def prior_out():
            nc.vector.tensor_copy(
                out=prior[:].rearrange("p (q c) -> p q c", c=4), in_=xt["prior"][:].rearrange("p c q -> p q c")
            )

        def load_uni(lo, hi):
            if lo % 4 == 0:
                t = raw.tile([P, 4, U], BF16, tag="uni_raw", bufs=3)
                uni_raw[lo // 4] = t
            nc.sync.dma_start(out=uni_raw[lo // 4][:, lo % 4 : lo % 4 + hi - lo, :], in_=uni_v[:, lo:hi, :])

        def load_bi(lo, hi):
            if lo % 2 == 0:
                t = raw.tile([P, 2, V], BF16, tag="bi_raw", bufs=5)
                bi_raw[lo // 2] = t
            nc.sync.dma_start(out=bi_raw[lo // 2][:, lo % 2 : lo % 2 + hi - lo, :], in_=bi_v[:, lo:hi, :])

        def load_gumbel(lo, hi):
            if lo % 8 == 0:
                t = raw.tile([P, 8, T], BF16, tag="gum", bufs=2)
                gum_raw[lo // 8] = t
            nc.sync.dma_start(out=gum_raw[lo // 8][:, lo % 8 : lo % 8 + hi - lo, :], in_=gumbel_v[:, lo:hi, :])

        def load_ratio(c):
            t = raw.tile([P, 4, T], BF16, tag="r_raw", bufs=4)
            src = uni_ratio_v[c] if c < UNI_PASSES else bi_ratio_v[c - UNI_PASSES]
            nc.sync.dma_start(out=t[:], in_=src)
            r_raw[c] = t

        def interleave(c, lo, hi, engine):
            if c not in r_grp:
                g = work.tile([P, T, 4], BF16, tag="r_grp", align_bytes=64)
                r_grp[c] = g
            dst = r_grp[c][:, lo:hi, :]
            src = r_raw[c][:, :, lo:hi].rearrange("p t w -> p w t")
            if engine == "V":
                nc.vector.tensor_copy(out=dst, in_=src)
            else:
                nc.scalar.copy(out=dst, in_=src)

        def quant_ratio(c):
            nc.vector.quantize_mx(
                out=ratio_codes[:, c, :].bitcast(E4M3),
                scales=ratio_scales[:, c, :],
                in_=r_grp[c][:].rearrange("p w t -> p (w t)"),
            )

        def words(i, g):
            if g < UNI_PASSES:
                return uni_raw[i // 4][:, i % 4, g * K_PASS : (g + 1) * K_PASS].bitcast(F32)
            return bi_raw[i // 2][:, i % 2, (g - UNI_PASSES) * K_PASS : (g - UNI_PASSES + 1) * K_PASS].bitcast(F32)

        def pack(i, lo, hi, engine):
            if i not in packed:
                t = work.tile([P, PASSES, 2, P], F32, tag="packed")
                packed[i] = t
            if hi <= UNI_PASSES:
                src = uni_raw[i // 4][:, i % 4, lo * K_PASS : hi * K_PASS]
            else:
                src = bi_raw[i // 2][:, i % 2, (lo - UNI_PASSES) * K_PASS : (hi - UNI_PASSES) * K_PASS]
            src = src.bitcast(F32).rearrange("p (g w u) -> p g u w", g=hi - lo, u=2)
            if engine == "S":
                nc.scalar.copy(out=packed[i][:, lo:hi, :, :], in_=src)
            else:
                nc.vector.tensor_copy(out=packed[i][:, lo:hi, :, :], in_=src)

        def transposes(i, b):
            x = psum_x.tile([P, 2, 2, P], F32, tag="xt")
            xt[i, b] = x
            for g in range(2):
                for u in range(2):
                    if i in packed:
                        src = packed[i][:, 2 * b + g, u, :]
                    else:
                        src = words(i, 2 * b + g)[:, u : 2 * P : 2]
                    nc.tensor.transpose(x[:, g, u, :], src, ident[:])

        def evac(i, b, engine="S"):
            if i not in grouped:
                t = work.tile([P, PASSES, 4 * P], BF16, tag="grouped", align_bytes=64, bufs=4)
                grouped[i] = t
            dst = grouped[i][:, 2 * b : 2 * b + 2, :].bitcast(F32).rearrange("p g (r u) -> p g r u", u=2)
            src = xt[i, b][:].rearrange("p g u r -> p g r u")
            if engine == "S":
                nc.scalar.copy(out=dst, in_=src)
            else:
                nc.vector.tensor_copy(out=dst, in_=src)

        def quant_counts(i, lo, hi):
            if i not in codes:
                c = work.tile([P, PASSES, P], U32, tag="codes", align_bytes=64, bufs=4)
                s = work.tile([P, PASSES, P], U8, tag="scales", align_bytes=64, bufs=4)
                codes[i], scales[i] = c, s
            nc.vector.quantize_mx(
                out=codes[i][:, lo:hi, :].rearrange("p g r -> p (g r)").bitcast(E4M3 if hi <= UNI_PASSES else E5M2),
                scales=scales[i][:, lo:hi, :].rearrange("p g r -> p (g r)"),
                in_=grouped[i][:, lo:hi, :].rearrange("p g c -> p (g c)"),
            )

        def quant_uni(i):
            quant_counts(i, 0, UNI_PASSES)

        def quant_bi(i):
            quant_counts(i, UNI_PASSES, PASSES)

        def product(i, c):
            if i not in acc:
                a = psum_a.tile([P, T], F32, tag="acc")
                acc[i] = a
            nc.tensor.matmul_mx(
                out=acc[i][:],
                lhsT=codes[i][:, c, :].bitcast(E4M3 if c < UNI_PASSES else E5M2),
                lhsT_scale=scales[i][:, c, :],
                rhs=ratio_codes[:, c, :].bitcast(E4M3),
                rhs_scale=ratio_scales[:, c, :],
                start=(c == 0),
                stop=(c == PASSES - 1),
            )

        def products(i):
            for c in range(PASSES):
                product(i, c)

        def log_weight(i):
            t = outs.tile([P, T], F32, tag="lw", bufs=5)
            lw[i] = t
            for lo, hi in parts(i):
                nc.vector.scalar_tensor_tensor(
                    out=t[:, lo:hi], in0=acc[i][:, lo:hi], scalar=gain[:, i : i + 1], in1=prior[:, lo:hi], op0=MULT, op1=ADD
                )

        def weight_exp(i):
            if i % 2 == 0:
                t = outs.tile([P, 2, T], F32, tag="w_out", bufs=4)
                w_pair[i // 2] = t
            for lo, hi in parts(i):
                nc.scalar.activation(w_pair[i // 2][:, i % 2, lo:hi], lw[i][:, lo:hi], ACT.Exp)

        def key_add(i):
            if i % 2 == 0:
                t = outs.tile([P, 2, T], F32, tag="k_out", bufs=4)
                k_pair[i // 2] = t
            nc.vector.tensor_tensor(
                out=k_pair[i // 2][:, i % 2, :], in0=lw[i][:], in1=gum_raw[i // 8][:, i % 8, :], op=ADD
            )

        def store(i):
            for lo, hi in STORES:
                if hi == i + 1:
                    a, b = lo % 2, lo % 2 + hi - lo
                    nc.sync.dma_start(out=weight_v[:, lo:hi, :], in_=w_pair[i // 2][:, a:b, :])
                    nc.sync.dma_start(out=key_v[:, lo:hi, :], in_=k_pair[i // 2][:, a:b, :])

        load_small()
        load_uni(0, 2)
        load_ratio(0)
        load_bi(0, 1)
        load_ratio(1)
        load_bi(1, 2)
        load_uni(2, 4)
        load_ratio(2)
        load_ratio(3)
        load_ratio(4)
        load_bi(2, 3)
        load_ratio(5)
        load_bi(3, 4)
        load_uni(4, 6)
        load_bi(4, 6)
        load_bi(6, 8)
        load_gumbel(0, 4)
        load_uni(6, 8)
        load_bi(8, 10)
        load_uni(8, 12)
        load_gumbel(4, 8)
        warm_exp()
        transposes(0, 0)
        transposes(1, 0)
        transposes(0, 1)
        transposes(0, 2)
        evac(0, 0)
        prep_small()
        transposes(1, 1)
        transposes(1, 2)
        evac(1, 0)
        quant_uni(0)
        interleave(0, 0, 304, "S")
        interleave(0, 304, 512, "V")
        evac(0, 1)
        prior_pe()
        interleave(1, 0, 64, "S")
        interleave(1, 64, 512, "V")
        transposes(2, 0)
        transposes(3, 0)
        evac(0, 2)
        evac(1, 1)
        quant_uni(1)
        quant_ratio(0)
        quant_ratio(1)
        quant_bi(0)
        product(0, 0)
        product(0, 1)
        product(1, 0)
        product(1, 1)
        evac(1, 2)
        prior_out()
        interleave(2, 0, 256, "S")
        interleave(2, 256, 512, "V")
        quant_bi(1)
        evac(2, 0)
        quant_uni(2)
        quant_ratio(2)
        evac(3, 0)
        interleave(3, 0, 304, "S")
        interleave(3, 304, 512, "V")
        quant_uni(3)
        product(0, 2)
        product(1, 2)
        quant_ratio(3)
        transposes(2, 1)
        transposes(2, 2)
        interleave(4, 0, 240, "S")
        interleave(4, 240, 512, "V")
        evac(2, 2)
        product(2, 0)
        product(2, 1)
        quant_ratio(4)
        interleave(5, 0, 128, "S")
        interleave(5, 128, 512, "V")
        evac(2, 1)
        product(0, 3)
        product(1, 3)
        transposes(3, 1)
        transposes(3, 2)
        evac(3, 1)
        quant_bi(2)
        quant_ratio(5)
        product(0, 4)
        product(1, 4)
        product(2, 2)
        product(2, 3)
        product(2, 4)
        evac(3, 2)
        pack(4, 0, 2, "S")
        product(0, 5)
        product(1, 5)
        product(2, 5)
        quant_bi(3)
        pack(4, 2, 6, "V")
        pack(5, 0, 2, "S")
        pack(5, 2, 6, "V")
        log_weight(0)
        log_weight(1)
        for s in range(4, TILES + 2):
            if s < TILES:
                for b in range(3):
                    transposes(s, b)
            if s - 1 < TILES:
                products(s - 1)
            if s % 2 == 0 and s + 6 < TILES:
                load_bi(s + 6, s + 8)
            if s % 4 == 0 and s + 8 < TILES:
                load_uni(s + 8, s + 12)
            if s == 6:
                load_gumbel(8, 16)
            log_weight(s - 2)
            if s < TILES:
                evac(s, 0)
                evac(s, 1)
                evac(s, 2)
                quant_uni(s)
            for i in KEYS[s]:
                weight_exp(i)
                key_add(i)
            if s < TILES:
                quant_bi(s)
            if s + 2 < TILES:
                pack(s + 2, 0, 2, "S" if s % 4 != 3 else "V")
                pack(s + 2, 2, 6, "V")
            for i in KEYS[s]:
                store(i)
